import numpy as np
import ml_dtypes


def mxq(x, axis, fmt="e4m3"):
    dtype, down = {"e4m3": (ml_dtypes.float8_e4m3fn, 7), "e5m2": (ml_dtypes.float8_e5m2, 14)}[fmt]
    v = np.moveaxis(np.asarray(x, np.float32).astype(ml_dtypes.bfloat16).astype(np.float64), axis, -1)
    blocks = v.reshape(v.shape[:-1] + (-1, 32))
    amax = np.abs(blocks).max(-1, keepdims=True)
    byte = np.maximum(np.where(amax > 0, np.frexp(amax)[1] - 1 + 127, 0) - down, 1)
    scale = np.exp2(byte - 127.0)
    codes = (blocks / scale).astype(np.float32).astype(dtype).astype(np.float64)
    return np.moveaxis((codes * scale).reshape(v.shape), -1, axis)


WIDE = False


def mx_kscale(k):
    if not WIDE:
        return np.ones(k)
    levels = np.array([10, -10, 5, -5, 0])
    if k % 512:
        return np.exp2(np.random.permutation(np.resize(levels, k // 32))).repeat(32)
    a = np.empty((k // 512, 16))
    for p in range(k // 512):
        a[p, :8] = np.random.permutation(np.resize(levels, 8))
        for g in range(8):
            far = levels[np.abs(levels - a[p, g]) >= 10]
            a[p, g + 8] = far[np.random.randint(len(far))]
    return np.exp2(a.ravel()).repeat(32)


def f64(x):
    return np.asarray(x).astype(np.float64)


def striped(idx):
    return np.tile(np.asarray(idx).reshape(-1, 16).T, (8, 1)).astype(np.uint16)


def unstriped(offs):
    return offs[:16].T.reshape(-1).astype(np.int64)


E2M1 = np.array([0.0, 0.5, 1.0, 1.5, 2.0, 3.0, 4.0, 6.0, -0.0, -0.5, -1.0, -1.5, -2.0, -3.0, -4.0, -6.0])


def pack_weight(w, fmt):
    k, n = w.shape
    w = f64(np.asarray(w, np.float32).astype(ml_dtypes.bfloat16)).reshape(k // 32, 32, n)
    amax = np.abs(w).max(1)
    if fmt == "e4m3":
        byte = np.frexp(amax)[1] - 1 + 127 - 7
    else:
        mant, ex = np.frexp(amax / 6.0)
        byte = np.where(mant > 0.5, ex, ex - 1) + 127
    byte = np.clip(np.where(amax > 0, byte, 1), 1, 254)
    scaled = (w * np.exp2(127.0 - byte)[:, None, :]).reshape(k, n).astype(np.float32)
    by_word = np.ascontiguousarray(scaled.reshape(k // 512, 128, 4, n).transpose(0, 1, 3, 2))
    if fmt == "e4m3":
        words = by_word.astype(ml_dtypes.float8_e4m3fn).view(np.uint8)
    else:
        c = by_word.astype(ml_dtypes.float4_e2m1fn).view(np.uint8) & 0xF
        words = (c[..., 0::2] | (c[..., 1::2] << 4)).reshape(k // 512, 128, 2 * n)
    return np.ascontiguousarray(words), np.ascontiguousarray(byte.astype(np.uint8).reshape(k // 512, 16, n))


def unpack_weight(words, scales, fmt):
    g, _, n = scales.shape
    words = np.ascontiguousarray(words).reshape(g, 128, n, -1)
    if fmt == "e4m3":
        vals = words.view(ml_dtypes.float8_e4m3fn).astype(np.float64)
    else:
        nib = np.empty((g, 128, n, 4), np.uint8)
        nib[..., 0::2] = words & 0xF
        nib[..., 1::2] = words >> 4
        vals = E2M1[nib]
    vals = vals * np.repeat(np.exp2(scales.astype(np.float64) - 127.0), 8, axis=1)[..., None]
    return vals.transpose(0, 1, 3, 2).reshape(g * 512, n)


K, T, J, N = 512, 2048, 512, 256


def setup_inputs():
    n = np.random.standard_normal
    idx = np.random.permutation(T)[:J]
    fk = mx_kscale(K)
    xqp = pack_weight(n((K, T)) / fk[:, None], "e2m1")
    wp = pack_weight(n((K, N)) * 1 / np.sqrt(K) * fk[:, None], "e2m1")
    wep = pack_weight(n((K, N)) * 1 / np.sqrt(K) * fk[:, None], "e4m3")
    return {
        "xq_words": xqp[0],
        "xq_scales": xqp[1],
        "w_words": wp[0],
        "w_scales": wp[1],
        "xf": (n((K, T)) / fk[:, None]).astype(np.float32),
        "xc": (n((K, T)) * 0.9 / fk[:, None]).astype(np.float32),
        "we_words": wep[0],
        "we_scales": wep[1],
        "offs": striped(idx),
    }


def reference(xq_words, xq_scales, w_words, w_scales, xf, xc, we_words, we_scales, offs):
    idx = unstriped(offs)
    xqu = unpack_weight(xq_words, xq_scales, "e2m1")
    wu = unpack_weight(w_words, w_scales, "e2m1")
    weu = unpack_weight(we_words, we_scales, "e4m3")
    z = wu.T @ xqu
    e = f64(xf)[:, idx] - f64(xc)[:, idx]
    eq = mxq(e, 0, "e4m3")
    p = weu.T @ eq
    d = np.tanh(p)
    dp = np.zeros((N, T))
    dp[:, idx] = d
    y = z + dp
    return y

from contextlib import ExitStack

import concourse.mybir as mybir

K, T, J, N = 512, 2048, 512, 256
FLOPS = 2 * K * N * (T + J)

F32 = mybir.dt.float32
BF16 = mybir.dt.bfloat16
I32 = mybir.dt.int32
U32 = mybir.dt.uint32
U16 = mybir.dt.uint16
U8 = mybir.dt.uint8
FP8X4 = mybir.dt.float8_e4m3fn_x4
FP4X4 = mybir.dt.float4_e2m1fn_x4
ACT = mybir.ActivationFunctionType
ALU = mybir.AluOpType

P = 128
PACK = 4
BANK = 512
PIECE = J // 2
LIST_COLS = PIECE // 16


def load_scale_rows(nc, plane, rows):
    for quad in range(4):
        nc.sync.dma_start(
            out=plane[32 * quad : 32 * quad + 4, :].bitcast(I32),
            in_=rows[4 * quad : 4 * quad + 4, :].bitcast(I32),
        )


def tile_list_error_feedback_lists_kernel(
    tc, xq_words, xq_scales, w_words, w_scales, xf, xc, we_words, we_scales, offs, out
):
    nc = tc.nc
    with ExitStack() as ctx:
        sb = ctx.enter_context(tc.tile_pool(name="sb", bufs=1))
        ps = ctx.enter_context(tc.psum_pool(name="ps", bufs=1))

        offsets = sb.tile([P, J // 16], U16, name="offsets")
        xf_planes = [sb.tile([P, T], F32, name="xf%d" % r) for r in range(PACK)]
        xc_planes = [sb.tile([P, T], F32, name="xc%d" % r) for r in range(PACK)]
        we_codes = sb.tile([P, N], U32, name="we_codes", align_bytes=64)
        we_plane = sb.tile([P, N], U8, name="we_plane", align_bytes=64)
        w_codes = sb.tile([P, 2 * N], U8, name="w_codes", align_bytes=64)
        w_plane = sb.tile([P, N], U8, name="w_plane", align_bytes=64)
        xq_codes = sb.tile([P, 2 * T], U8, name="xq_codes", align_bytes=64)
        xq_plane = sb.tile([P, T], U8, name="xq_plane", align_bytes=64)
        placed = [sb.tile([P, T], F32, name="placed%d" % h) for h in range(2)]

        for plane in (we_plane, w_plane, xq_plane):
            nc.vector.memset(plane[:].bitcast(I32), 0)
        for h in range(2):
            nc.vector.memset(placed[h][:], 0.0)

        xf_rows = xf.rearrange("(p r) t -> p r t", r=PACK)
        xc_rows = xc.rearrange("(p r) t -> p r t", r=PACK)
        for r in range(PACK):
            nc.sync.dma_start(out=xc_planes[r][:], in_=xc_rows[:, r, :])
            if r == 0:
                nc.sync.dma_start(offsets[:], offs)
            nc.sync.dma_start(out=xf_planes[r][:], in_=xf_rows[:, r, :])
        nc.sync.dma_start(
            out=we_codes[:].bitcast(I32),
            in_=we_words[0].rearrange("p n r -> p (n r)").bitcast(I32),
        )
        load_scale_rows(nc, we_plane, we_scales[0])
        nc.sync.dma_start(out=xq_codes[:].bitcast(I32), in_=xq_words[0].bitcast(I32))
        nc.sync.dma_start(out=w_codes[:].bitcast(I32), in_=w_words[0].bitcast(I32))
        load_scale_rows(nc, w_plane, w_scales[0])
        load_scale_rows(nc, xq_plane, xq_scales[0])

        def entries(s):
            return slice(s * PIECE, (s + 1) * PIECE)

        def listed(tile, s):
            return tile[:].indirect(offsets[:, s * LIST_COLS : (s + 1) * LIST_COLS])

        grouped = [sb.tile([P, PIECE, PACK], BF16, name="grouped%d" % s, align_bytes=64) for s in range(2)]
        e_codes = sb.tile([P, J], U32, name="e_codes", align_bytes=64)
        e_plane = sb.tile([P, J], U8, name="e_plane", align_bytes=64)

        last = PACK - 1
        for r in range(PACK):
            coarse = sb.tile([P, J], F32, name="coarse%d" % r)
            nc.scalar.activation(coarse[:], xc_planes[r][:].indirect(offsets[:]), ACT.Copy)
            if r < last:
                diff = sb.tile([P, J], F32, name="diff%d" % r)
                nc.vector.tensor_tensor(diff[:], xf_planes[r][:].indirect(offsets[:]), coarse[:], ALU.subtract)
                for s in range(2):
                    nc.vector.tensor_copy(grouped[s][:, :, r], diff[:, entries(s)])
            else:
                diff_a = sb.tile([P, PIECE], F32, name="diff_a")
                fine_b = sb.tile([P, PIECE], F32, name="fine_b")
                diff_b = sb.tile([P, PIECE], F32, name="diff_b")
                nc.scalar.activation(fine_b[:], listed(xf_planes[r], 1), ACT.Copy)
                nc.vector.tensor_tensor(diff_a[:], listed(xf_planes[r], 0), coarse[:, entries(0)], ALU.subtract)
                nc.vector.tensor_copy(grouped[0][:, :, r], diff_a[:])
                nc.vector.tensor_tensor(diff_b[:], fine_b[:], coarse[:, entries(1)], ALU.subtract)
                nc.vector.quantize_mx(
                    out=e_codes[:, entries(0)].bitcast(FP8X4),
                    scales=e_plane[:, entries(0)],
                    in_=grouped[0][:].rearrange("p j r -> p (j r)"),
                )
                nc.vector.tensor_copy(grouped[1][:, :, r], diff_b[:])
                nc.vector.quantize_mx(
                    out=e_codes[:, entries(1)].bitcast(FP8X4),
                    scales=e_plane[:, entries(1)],
                    in_=grouped[1][:].rearrange("p j r -> p (j r)"),
                )

        def feedback_matmul(dst, h, cols):
            rows = slice(h * P, (h + 1) * P)
            nc.tensor.matmul_mx(
                out=dst,
                lhsT=we_codes[:, rows].bitcast(FP8X4),
                lhsT_scale=we_plane[:, rows],
                rhs=e_codes[:, cols].bitcast(FP8X4),
                rhs_scale=e_plane[:, cols],
                start=True,
                stop=True,
            )

        p_low = [ps.tile([P, PIECE], F32, name="p_low%d" % s, tag="bank%d" % (5 + s)) for s in range(2)]
        p_high = ps.tile([P, J], F32, name="p_high", tag="bank7")
        d_low = [sb.tile([P, PIECE], F32, name="d_low%d" % s) for s in range(2)]
        d_high = sb.tile([P, J], F32, name="d_high")
        for s in range(2):
            feedback_matmul(p_low[s][:], 0, entries(s))
        feedback_matmul(p_high[:], 1, slice(0, J))
        for s in range(2):
            nc.scalar.activation(d_low[s][:], p_low[s][:], ACT.Tanh)
        nc.scalar.activation(d_high[:], p_high[:], ACT.Tanh)
        for s in range(2):
            nc.vector.tensor_copy(listed(placed[0], s), d_low[s][:])
        for s in range(2):
            nc.scalar.activation(listed(placed[1], s), d_high[:, entries(s)], ACT.Copy)

        for h in range(2):
            z = [ps.tile([P, BANK], F32, name="z%d_%d" % (h, c), tag="bank%d" % (4 * h + c)) for c in range(T // BANK)]
            for c in range(T // BANK):
                nc.tensor.matmul_mx(
                    out=z[c][:],
                    lhsT=w_codes[:, 2 * P * h : 2 * P * (h + 1)].bitcast(FP4X4),
                    lhsT_scale=w_plane[:, P * h : P * (h + 1)],
                    rhs=xq_codes[:, 2 * BANK * c : 2 * BANK * (c + 1)].bitcast(FP4X4),
                    rhs_scale=xq_plane[:, BANK * c : BANK * (c + 1)],
                    start=True,
                    stop=True,
                )
            for c in range(T // BANK):
                cols = slice(BANK * c, BANK * (c + 1))
                result = sb.tile([P, BANK], F32, name="result%d_%d" % (h, c))
                nc.vector.tensor_tensor(result[:], z[c][:], placed[h][:, cols], ALU.add)
                nc.sync.dma_start(out=out[P * h : P * (h + 1), cols], in_=result[:])
